import numpy as np
import ml_dtypes


def mxq(x, axis, fmt="e4m3"):
    dtype, down = {"e4m3": (ml_dtypes.float8_e4m3fn, 7), "e5m2": (ml_dtypes.float8_e5m2, 14)}[fmt]
    v = np.moveaxis(np.asarray(x, np.float32).astype(ml_dtypes.bfloat16).astype(np.float64), axis, -1)
    blocks = v.reshape(v.shape[:-1] + (-1, 32))
    amax = np.abs(blocks).max(-1, keepdims=True)
    byte = np.maximum(np.where(amax > 0, np.frexp(amax)[1] - 1 + 127, 0) - down, 1)
    scale = np.exp2(byte - 127.0)
    codes = (blocks / scale).astype(np.float32).astype(dtype).astype(np.float64)
    return np.moveaxis((codes * scale).reshape(v.shape), -1, axis)


WIDE = False


def mx_kscale(k):
    if not WIDE:
        return np.ones(k)
    levels = np.array([10, -10, 5, -5, 0])
    if k % 512:
        return np.exp2(np.random.permutation(np.resize(levels, k // 32))).repeat(32)
    a = np.empty((k // 512, 16))
    for p in range(k // 512):
        a[p, :8] = np.random.permutation(np.resize(levels, 8))
        for g in range(8):
            far = levels[np.abs(levels - a[p, g]) >= 10]
            a[p, g + 8] = far[np.random.randint(len(far))]
    return np.exp2(a.ravel()).repeat(32)


BF16 = ml_dtypes.bfloat16


def bf(x):
    return np.asarray(x, np.float32).astype(BF16)


def f64(x):
    return np.asarray(x).astype(np.float64)


E2M1 = np.array([0.0, 0.5, 1.0, 1.5, 2.0, 3.0, 4.0, 6.0, -0.0, -0.5, -1.0, -1.5, -2.0, -3.0, -4.0, -6.0])


def pack_weight(w, fmt):
    k, n = w.shape
    w = f64(bf(w)).reshape(k // 32, 32, n)
    amax = np.abs(w).max(1)
    if fmt == "e4m3":
        byte = np.frexp(amax)[1] - 1 + 127 - 7
    else:
        mant, ex = np.frexp(amax / 6.0)
        byte = np.where(mant > 0.5, ex, ex - 1) + 127
    byte = np.clip(np.where(amax > 0, byte, 1), 1, 254)
    scaled = (w * np.exp2(127.0 - byte)[:, None, :]).reshape(k, n).astype(np.float32)
    by_word = np.ascontiguousarray(scaled.reshape(k // 512, 128, 4, n).transpose(0, 1, 3, 2))
    if fmt == "e4m3":
        words = by_word.astype(ml_dtypes.float8_e4m3fn).view(np.uint8)
    else:
        c = by_word.astype(ml_dtypes.float4_e2m1fn).view(np.uint8) & 0xF
        words = c[..., 0::2] | (c[..., 1::2] << 4)
    return np.ascontiguousarray(words), np.ascontiguousarray(byte.astype(np.uint8).reshape(k // 512, 16, n))


def unpack_weight(words, scales, fmt):
    g, p, n, _ = words.shape
    if fmt == "e4m3":
        vals = np.ascontiguousarray(words).view(ml_dtypes.float8_e4m3fn).astype(np.float64)
    else:
        nib = np.empty((g, p, n, 4), np.uint8)
        nib[..., 0::2] = words & 0xF
        nib[..., 1::2] = words >> 4
        vals = E2M1[nib]
    vals = vals * np.repeat(np.exp2(scales.astype(np.float64) - 127.0), 8, axis=1)[..., None]
    return vals.transpose(0, 1, 3, 2).reshape(g * 512, n)

E4M3FN = np.array([(-1.0 if i & 128 else 1.0) * ((1.0 + (i & 7) / 8.0) * 2.0 ** (((i >> 3) & 15) - 7) if i & 120 else (i & 7) * 2.0 ** -9) for i in range(256)])


def e4m3fn_bytes(y):
    return np.clip(np.asarray(y, np.float64), -448.0, 448.0).astype(np.float32).astype(ml_dtypes.float8_e4m3fn).view(np.uint8)


def e4m3fn_values(b):
    return E4M3FN[b]


S, P, M = 1024, 512, 1024


def draw0():
    a, c = mx_kscale(S), mx_kscale(P)
    r = bf(np.random.standard_normal((S, M)) * a[:, None])
    v = bf(np.random.standard_normal((P, M)) * c[:, None])
    finv = bf(np.random.uniform(0.5, 1.5, P))
    k_words, k_scales = pack_weight(np.random.standard_normal((S, P)) / np.sqrt(S) / a[:, None] * c[None, :], "e4m3")
    z_words, z_scales = pack_weight(np.random.standard_normal((P, S)) / np.sqrt(P) / c[:, None], "e4m3")
    t_words, t_scales = pack_weight(np.random.standard_normal((S, S)) / np.sqrt(S) / a[:, None], "e4m3")
    h = bf(np.random.uniform(0.5, 1.5, P) / c)
    return {
        "r": r,
        "v": v,
        "finv": finv,
        "k_words": k_words,
        "k_scales": k_scales,
        "z_words": z_words,
        "z_scales": z_scales,
        "t_words": t_words,
        "t_scales": t_scales,
        "h": h,
    }


def core(r, v, finv, k_words, k_scales, z_words, z_scales, t_words, t_scales, h):
    rq = mxq(f64(r), 0, "e4m3")
    kr = unpack_weight(k_words, k_scales, "e4m3").T @ rq
    u = f64(finv)[:, None] * f64(v) - kr
    zu = unpack_weight(z_words, z_scales, "e4m3").T @ mxq(u, 0, "e4m3")
    tr = unpack_weight(t_words, t_scales, "e4m3").T @ rq
    r_prev = zu + tr
    eps = f64(h)[:, None] * u
    return r_prev, eps


def setup_inputs():
    drawn = draw0()
    full = np.asarray(drawn['r']).astype(np.float64)
    scale = (np.abs(full).reshape(1024, 8, 128).max(axis=(2,)) / 448.0).astype(np.float32)
    given = {}
    for key, value in drawn.items():
        if key == 'r':
            given['r_bytes'] = e4m3fn_bytes(full / np.repeat(scale.astype(np.float64), 128, axis=1))
            given['r_scale'] = scale
        else:
            given[key] = value
    return given


def reference(r_bytes, r_scale, v, finv, k_words, k_scales, z_words, z_scales, t_words, t_scales, h):
    return core(e4m3fn_values(r_bytes) * np.repeat(r_scale.astype(np.float64), 128, axis=1), v, finv, k_words, k_scales, z_words, z_scales, t_words, t_scales, h)

@@ -1,0 +1,281 @@
+from contextlib import ExitStack
+
+import concourse.mybir as mybir
+
+S, P_OBS, M = 1024, 512, 1024
+FLOPS = 2 * M * (2 * S * P_OBS + S * S)
+
+F32 = mybir.dt.float32
+BF16 = mybir.dt.bfloat16
+I32 = mybir.dt.int32
+U32 = mybir.dt.uint32
+U8 = mybir.dt.uint8
+FP8 = mybir.dt.float8_e4m3fn
+FP8X4 = mybir.dt.float8_e4m3fn_x4
+COPY = mybir.ActivationFunctionType.Copy
+MULT = mybir.AluOpType.mult
+SUB = mybir.AluOpType.subtract
+
+P = 128
+PACK = 4
+BLOCK = 128
+BANK = 512
+
+WIDTHS = (128, 128, 256, 256, 128, 128)
+SLICES = (4, 4, 2, 2, 4, 2)
+
+
+def tile_durbinkoopmandisturbancesmootherstep_d1p_kernel(
+    tc, r_bytes, r_scale, v, finv, k_words, k_scales, z_words, z_scales, t_words, t_scales, h, out_0, out_1
+):
+    nc = tc.nc
+    starts = [sum(WIDTHS[:c]) for c in range(len(WIDTHS))]
+    n_chunks = len(WIDTHS)
+
+    r_view = r_bytes.rearrange("(g p t) m -> p g t m", p=P, t=PACK)
+    v_view = v.rearrange("(p t) m -> p t m", t=PACK)
+    eps_view = out_1.rearrange("(p t) m -> p t m", t=PACK)
+    prev_view = out_0.rearrange("(s p) m -> p s m", p=P)
+
+    with ExitStack() as ctx:
+        keep = ctx.enter_context(tc.tile_pool(name="keep", bufs=1))
+        psum = ctx.enter_context(tc.psum_pool(name="psum", bufs=8))
+
+        ctx.enter_context(tc.manual_schedule())
+
+        r_raw = keep.tile([P, 2, PACK, M], U8, name="r_raw", align_bytes=64)
+        r_sc = keep.tile([P, 2, PACK, M // BLOCK], F32, name="r_sc", align_bytes=64)
+        v_sb = keep.tile([P, PACK, M], BF16, name="v_sb", align_bytes=64)
+        vec_bf = keep.tile([P, 2, 16], BF16, name="vec_bf", align_bytes=64)
+        vec = keep.tile([P, 2, PACK], F32, name="vec", align_bytes=64)
+        k_raw = keep.tile([P, 2, P_OBS], U32, name="k_raw", align_bytes=64)
+        k_codes = keep.tile([P, 2, P_OBS], U32, name="k_codes", align_bytes=64)
+        ks_raw = keep.tile([P, P_OBS], U8, name="ks_raw", align_bytes=64)
+        k_sc = keep.tile([P, P_OBS], U8, name="k_sc", align_bytes=64)
+        t_codes = keep.tile([P, 2, S], U32, name="t_codes", align_bytes=64)
+        z_codes = keep.tile([P, S], U32, name="z_codes", align_bytes=64)
+        t_sc = keep.tile([P, S], U8, name="t_sc", align_bytes=64)
+        z_sc = keep.tile([P, S], U8, name="z_sc", align_bytes=64)
+
+        for plane in (ks_raw, t_sc, z_sc):
+            nc.vector.memset(plane[:].bitcast(U32), 0)
+
+        k_dram = k_words.rearrange("g p n t -> p g (n t)").bitcast(I32)
+        t_dram = t_words.rearrange("g p n t -> p g (n t)").bitcast(I32)
+        z_dram = z_words[0].rearrange("p n t -> p (n t)").bitcast(I32)
+        nc.sync.dma_start(out=r_sc[:], in_=r_scale.rearrange("(g p t) j -> p g t j", p=P, t=PACK))
+        for g in range(2):
+            nc.sync.dma_start(out=r_raw[:, g, :, 0:512], in_=r_view[:, g, :, 0:512])
+        for q in range(4):
+            nc.scalar.dma_start(
+                out=ks_raw[32 * q : 32 * q + 8, :].bitcast(I32), in_=k_scales[:, 4 * q : 4 * q + 4, :].bitcast(I32)
+            )
+        for q in range(4):
+            nc.gpsimd.dma_start(
+                out=t_sc[32 * q : 32 * q + 8, :].bitcast(I32), in_=t_scales[:, 4 * q : 4 * q + 4, :].bitcast(I32)
+            )
+        nc.gpsimd.dma_start(out=vec_bf[:, 0, 0:PACK], in_=finv.rearrange("(p t) -> p t", t=PACK))
+        nc.gpsimd.dma_start(out=vec_bf[:, 1, 0:PACK], in_=h.rearrange("(p t) -> p t", t=PACK))
+        nc.sync.dma_start(out=k_raw[:].bitcast(I32), in_=k_dram)
+        nc.sync.dma_start(out=v_sb[:, :, 0:256], in_=v_view[:, :, 0:256])
+        nc.sync.dma_start(out=t_codes[:, 0, :].bitcast(I32), in_=t_dram[:, 0, :])
+        nc.sync.dma_start(out=t_codes[:, 1, :].bitcast(I32), in_=t_dram[:, 1, :])
+        for g in range(2):
+            nc.sync.dma_start(out=r_raw[:, g, :, 512:1024], in_=r_view[:, g, :, 512:1024])
+        for q in range(4):
+            nc.sync.dma_start(
+                out=z_sc[32 * q : 32 * q + 4, :].bitcast(I32), in_=z_scales[0, 4 * q : 4 * q + 4, :].bitcast(I32)
+            )
+        nc.sync.dma_start(out=z_codes[:].bitcast(I32), in_=z_dram)
+        nc.sync.dma_start(out=v_sb[:, :, 256:1024], in_=v_view[:, :, 256:1024])
+
+        wide, mixed, r_codes, r_planes = [], [], [], []
+        u32, u_mixed, u_codes, u_planes, eps = [], [], [], [], []
+        for c in range(n_chunks):
+            w = WIDTHS[c]
+            wide.append(keep.tile([P, 2, PACK, w], BF16, name="wide%d" % c, align_bytes=64))
+            mixed.append(keep.tile([P, 2, w, PACK], BF16, name="mixed%d" % c, align_bytes=64))
+            r_codes.append(keep.tile([P, 2 * w], U32, name="r_codes%d" % c, align_bytes=64))
+            r_planes.append(keep.tile([P, 2 * w], U8, name="r_planes%d" % c, align_bytes=64))
+            u32.append(keep.tile([P, PACK, w], F32, name="u32_%d" % c, align_bytes=64))
+            u_mixed.append(keep.tile([P, w, PACK], BF16, name="u_mixed%d" % c, align_bytes=64))
+            u_codes.append(keep.tile([P, w], U32, name="u_codes%d" % c, align_bytes=64))
+            u_planes.append(keep.tile([P, w], U8, name="u_planes%d" % c, align_bytes=64))
+            eps.append(keep.tile([P, PACK, w], F32, name="eps%d" % c, align_bytes=64))
+
+        def widen(c, g, on_vector):
+            for t in range(PACK):
+                for b in range(WIDTHS[c] // BLOCK):
+                    lo = starts[c] + b * BLOCK
+                    src = r_raw[:, g, t, lo : lo + BLOCK].bitcast(FP8)
+                    dst = wide[c][:, g, t, b * BLOCK : (b + 1) * BLOCK]
+                    sc = r_sc[:, g, t, lo // BLOCK : lo // BLOCK + 1]
+                    if on_vector:
+                        nc.vector.tensor_scalar(out=dst, in0=src, scalar1=sc, scalar2=None, op0=MULT)
+                    else:
+                        nc.scalar.activation(out=dst, in_=src, func=COPY, scale=sc)
+
+        def mix_r(c, g):
+            nc.vector.tensor_copy(out=mixed[c][:, g], in_=wide[c][:, g].rearrange("p t n -> p n t"))
+
+        def quant_r(c):
+            nc.vector.quantize_mx(
+                out=r_codes[c][:].bitcast(FP8X4),
+                scales=r_planes[c][:],
+                in_=mixed[c][:].rearrange("p g n t -> p (g n t)"),
+            )
+
+        kr = {}
+
+        def gain(c):
+            w = WIDTHS[c]
+            per = BANK // w
+            for b in range(PACK // per):
+                bank = psum.tile([P, per, w], F32, name="bank")
+                kr[c, b] = bank
+                for i in range(per):
+                    t = b * per + i
+                    for g in range(2):
+                        cols = slice(t * P, (t + 1) * P)
+                        nc.tensor.matmul_mx(
+                            out=bank[:, i, :],
+                            lhsT=k_codes[:, g, cols].bitcast(FP8X4),
+                            lhsT_scale=k_sc[4 * g : P, cols],
+                            rhs=r_codes[c][:, g * w : (g + 1) * w].bitcast(FP8X4),
+                            rhs_scale=r_planes[c][:, g * w : (g + 1) * w],
+                            start=(g == 0),
+                            stop=(g == 1),
+                        )
+
+        def error(c):
+            w = WIDTHS[c]
+            per = BANK // w
+            for t in range(PACK):
+                nc.vector.scalar_tensor_tensor(
+                    out=u32[c][:, t, :],
+                    in0=v_sb[:, t, starts[c] : starts[c] + w],
+                    scalar=vec[:, 0, t : t + 1],
+                    in1=kr[c, t // per][:, t % per, :],
+                    op0=MULT,
+                    op1=SUB,
+                )
+
+        def mix_u(c):
+            nc.vector.tensor_copy(out=u_mixed[c][:], in_=u32[c][:].rearrange("p t n -> p n t"))
+
+        def quant_u(c):
+            nc.vector.quantize_mx(
+                out=u_codes[c][:].bitcast(FP8X4),
+                scales=u_planes[c][:],
+                in_=u_mixed[c][:].rearrange("p n t -> p (n t)"),
+            )
+
+        def disturbance(c, ts, on_vector):
+            for t in ts:
+                if on_vector:
+                    nc.vector.tensor_scalar(
+                        out=eps[c][:, t, :], in0=u32[c][:, t, :], scalar1=vec[:, 1, t : t + 1], scalar2=None, op0=MULT
+                    )
+                else:
+                    nc.scalar.activation(out=eps[c][:, t, :], in_=u32[c][:, t, :], func=COPY, scale=vec[:, 1, t : t + 1])
+
+        def store_eps(c):
+            nc.sync.dma_start(out=eps_view[:, :, starts[c] : starts[c] + WIDTHS[c]], in_=eps[c][:])
+
+        acc = {}
+
+        def transition(c, b, i):
+            w = WIDTHS[c]
+            s = b * SLICES[c] + i
+            cols = slice(s * P, (s + 1) * P)
+            for g in range(2):
+                nc.tensor.matmul_mx(
+                    out=acc[c, b][:, i, :],
+                    lhsT=t_codes[:, g, cols].bitcast(FP8X4),
+                    lhsT_scale=t_sc[4 * g : P, cols],
+                    rhs=r_codes[c][:, g * w : (g + 1) * w].bitcast(FP8X4),
+                    rhs_scale=r_planes[c][:, g * w : (g + 1) * w],
+                    start=(g == 0),
+                    stop=False,
+                )
+
+        def observe(c, b, i):
+            w = WIDTHS[c]
+            s = b * SLICES[c] + i
+            cols = slice(s * P, (s + 1) * P)
+            nc.tensor.matmul_mx(
+                out=acc[c, b][:, i, :],
+                lhsT=z_codes[:, cols].bitcast(FP8X4),
+                lhsT_scale=z_sc[:, cols],
+                rhs=u_codes[c][:].bitcast(FP8X4),
+                rhs_scale=u_planes[c][:],
+                start=False,
+                stop=True,
+            )
+
+        def early(c):
+            w = WIDTHS[c]
+            per = SLICES[c]
+            for b in range(8 // per):
+                acc[c, b] = psum.tile([P, per, w], F32, name="bank")
+                transition(c, b, 0)
+
+        def late(c, vector_banks):
+            w = WIDTHS[c]
+            per = SLICES[c]
+            for b in range(8 // per):
+                observe(c, b, 0)
+                for i in range(1, per):
+                    transition(c, b, i)
+                    observe(c, b, i)
+                res = keep.tile([P, per, w], F32, name="res%d_%d" % (c, b), align_bytes=64)
+                if b in vector_banks:
+                    nc.vector.tensor_copy(out=res[:], in_=acc[c, b][:])
+                else:
+                    nc.scalar.copy(out=res[:], in_=acc[c, b][:])
+                nc.sync.dma_start(
+                    out=prev_view[:, b * per : (b + 1) * per, starts[c] : starts[c] + w], in_=res[:]
+                )
+
+        widen(0, 0, True)
+        widen(0, 1, False)
+        mix_r(0, 0)
+        mix_r(0, 1)
+        widen(1, 0, False)
+        widen(1, 1, False)
+        nc.vector.tensor_copy(
+            out=k_sc[:].rearrange("p (t m) -> p t m", t=PACK), in_=ks_raw[:].rearrange("p (m t) -> p t m", t=PACK)
+        )
+        nc.vector.tensor_copy(
+            out=k_codes[:].rearrange("p g (t m) -> p g t m", t=PACK).bitcast(I32),
+            in_=k_raw[:].bitcast(I32).rearrange("p g (m t) -> p g t m", t=PACK),
+        )
+        quant_r(0)
+        gain(0)
+        mix_r(1, 0)
+        mix_r(1, 1)
+        nc.vector.tensor_copy(out=vec[:], in_=vec_bf[:, :, 0:PACK])
+        widen(2, 0, False)
+        widen(2, 1, False)
+        early(0)
+        for c in range(n_chunks):
+            nxt = c + 1
+            error(c)
+            if nxt < n_chunks:
+                quant_r(nxt)
+                gain(nxt)
+            mix_u(c)
+            disturbance(c, (0, 1), True)
+            quant_u(c)
+            disturbance(c, (2, 3), False)
+            store_eps(c)
+            if c + 3 < n_chunks:
+                widen(c + 3, 0, False)
+            late(c, (0, 2) if c == n_chunks - 1 else ())
+            if nxt < n_chunks:
+                early(nxt)
+            if c + 2 < n_chunks:
+                mix_r(c + 2, 0)
+                mix_r(c + 2, 1)
+            if c + 3 < n_chunks:
+                widen(c + 3, 1, False)

@@ -21,16 +21,26 @@ PACK = 4
 BLOCK = 128
 BANK = 512
 
-WIDTHS = (128, 128, 256, 256, 128, 128)
-SLICES = (4, 4, 2, 2, 4, 2)
+GROUPS = ((256,), (256,), (256,), (256,))
+SLICES = (2, 2, 2, 2)
 
 
 def tile_durbinkoopmandisturbancesmootherstep_d1p_kernel(
     tc, r_bytes, r_scale, v, finv, k_words, k_scales, z_words, z_scales, t_words, t_scales, h, out_0, out_1
 ):
     nc = tc.nc
-    starts = [sum(WIDTHS[:c]) for c in range(len(WIDTHS))]
-    n_chunks = len(WIDTHS)
+    chunks = []
+    group_start, group_width = [], []
+    at = 0
+    for gi, parts in enumerate(GROUPS):
+        group_start.append(at)
+        group_width.append(sum(parts))
+        off = 0
+        for w in parts:
+            chunks.append((gi, off, w, at))
+            off += w
+            at += w
+    n_chunks = len(chunks)
 
     r_view = r_bytes.rearrange("(g p t) m -> p g t m", p=P, t=PACK)
     v_view = v.rearrange("(p t) m -> p t m", t=PACK)
@@ -40,7 +50,6 @@ def tile_durbinkoopmandisturbancesmootherstep_d1p_kernel(
     with ExitStack() as ctx:
         keep = ctx.enter_context(tc.tile_pool(name="keep", bufs=1))
         psum = ctx.enter_context(tc.psum_pool(name="psum", bufs=8))
-
         ctx.enter_context(tc.manual_schedule())
 
         r_raw = keep.tile([P, 2, PACK, M], U8, name="r_raw", align_bytes=64)
@@ -59,223 +68,279 @@ def tile_durbinkoopmandisturbancesmootherstep_d1p_kernel(
 
         for plane in (ks_raw, t_sc, z_sc):
             nc.vector.memset(plane[:].bitcast(U32), 0)
-
         k_dram = k_words.rearrange("g p n t -> p g (n t)").bitcast(I32)
         t_dram = t_words.rearrange("g p n t -> p g (n t)").bitcast(I32)
         z_dram = z_words[0].rearrange("p n t -> p (n t)").bitcast(I32)
-        nc.sync.dma_start(out=r_sc[:], in_=r_scale.rearrange("(g p t) j -> p g t j", p=P, t=PACK))
-        for g in range(2):
-            nc.sync.dma_start(out=r_raw[:, g, :, 0:512], in_=r_view[:, g, :, 0:512])
-        for q in range(4):
-            nc.scalar.dma_start(
+
+        def load_ks(queue, q):
+            queue.dma_start(
                 out=ks_raw[32 * q : 32 * q + 8, :].bitcast(I32), in_=k_scales[:, 4 * q : 4 * q + 4, :].bitcast(I32)
             )
-        for q in range(4):
-            nc.gpsimd.dma_start(
+
+        def load_ts(queue, q):
+            queue.dma_start(
                 out=t_sc[32 * q : 32 * q + 8, :].bitcast(I32), in_=t_scales[:, 4 * q : 4 * q + 4, :].bitcast(I32)
             )
-        nc.gpsimd.dma_start(out=vec_bf[:, 0, 0:PACK], in_=finv.rearrange("(p t) -> p t", t=PACK))
-        nc.gpsimd.dma_start(out=vec_bf[:, 1, 0:PACK], in_=h.rearrange("(p t) -> p t", t=PACK))
-        nc.sync.dma_start(out=k_raw[:].bitcast(I32), in_=k_dram)
-        nc.sync.dma_start(out=v_sb[:, :, 0:256], in_=v_view[:, :, 0:256])
-        nc.sync.dma_start(out=t_codes[:, 0, :].bitcast(I32), in_=t_dram[:, 0, :])
-        nc.sync.dma_start(out=t_codes[:, 1, :].bitcast(I32), in_=t_dram[:, 1, :])
-        for g in range(2):
-            nc.sync.dma_start(out=r_raw[:, g, :, 512:1024], in_=r_view[:, g, :, 512:1024])
-        for q in range(4):
-            nc.sync.dma_start(
+
+        def load_zs(queue, q):
+            queue.dma_start(
                 out=z_sc[32 * q : 32 * q + 4, :].bitcast(I32), in_=z_scales[0, 4 * q : 4 * q + 4, :].bitcast(I32)
             )
+
+        def load_vec(queue, i, src):
+            queue.dma_start(out=vec_bf[:, i, 0:PACK], in_=src.rearrange("(p t) -> p t", t=PACK))
+
+        for q in range(4):
+            load_ks(nc.gpsimd, q)
+        nc.sync.dma_start(out=r_sc[:], in_=r_scale.rearrange("(g p t) j -> p g t j", p=P, t=PACK))
+        nc.sync.dma_start(out=r_raw[:, 0], in_=r_view[:, 0])
+        nc.sync.dma_start(out=r_raw[:, 1], in_=r_view[:, 1])
+        nc.sync.dma_start(out=k_raw[:].bitcast(I32), in_=k_dram)
+        nc.sync.dma_start(out=v_sb[:, :, 0:512], in_=v_view[:, :, 0:512])
+        load_vec(nc.scalar, 0, finv)
+        load_vec(nc.scalar, 1, h)
+        nc.sync.dma_start(out=t_codes[:].bitcast(I32), in_=t_dram)
+        for q in range(4):
+            load_ts(nc.sync, q)
         nc.sync.dma_start(out=z_codes[:].bitcast(I32), in_=z_dram)
-        nc.sync.dma_start(out=v_sb[:, :, 256:1024], in_=v_view[:, :, 256:1024])
+        for q in range(4):
+            load_zs(nc.sync, q)
+        nc.sync.dma_start(out=v_sb[:, :, 512:1024], in_=v_view[:, :, 512:1024])
 
-        wide, mixed, r_codes, r_planes = [], [], [], []
-        u32, u_mixed, u_codes, u_planes, eps = [], [], [], [], []
-        for c in range(n_chunks):
-            w = WIDTHS[c]
-            wide.append(keep.tile([P, 2, PACK, w], BF16, name="wide%d" % c, align_bytes=64))
-            mixed.append(keep.tile([P, 2, w, PACK], BF16, name="mixed%d" % c, align_bytes=64))
-            r_codes.append(keep.tile([P, 2 * w], U32, name="r_codes%d" % c, align_bytes=64))
-            r_planes.append(keep.tile([P, 2 * w], U8, name="r_planes%d" % c, align_bytes=64))
-            u32.append(keep.tile([P, PACK, w], F32, name="u32_%d" % c, align_bytes=64))
-            u_mixed.append(keep.tile([P, w, PACK], BF16, name="u_mixed%d" % c, align_bytes=64))
-            u_codes.append(keep.tile([P, w], U32, name="u_codes%d" % c, align_bytes=64))
-            u_planes.append(keep.tile([P, w], U8, name="u_planes%d" % c, align_bytes=64))
-            eps.append(keep.tile([P, PACK, w], F32, name="eps%d" % c, align_bytes=64))
+        wide, mixed, r_codes, r_planes = {}, {}, [], []
+        u32, u_mixed, u_codes, u_planes, eps = [], {}, [], [], []
+        for gi, w in enumerate(group_width):
+            r_codes.append(keep.tile([P, 2, w], U32, name="r_codes%d" % gi, align_bytes=64))
+            r_planes.append(keep.tile([P, 2, w], U8, name="r_planes%d" % gi, align_bytes=64))
+            u32.append(keep.tile([P, PACK, w], F32, name="u32_%d" % gi, align_bytes=64))
+            u_codes.append(keep.tile([P, w], U32, name="u_codes%d" % gi, align_bytes=64))
+            u_planes.append(keep.tile([P, w], U8, name="u_planes%d" % gi, align_bytes=64))
+            eps.append(keep.tile([P, PACK, w], F32, name="eps%d" % gi, align_bytes=64))
+        for f, (gi, off, w, lo) in enumerate(chunks):
+            u_mixed[f] = keep.tile([P, w, PACK], BF16, name="u_mixed%d" % f, align_bytes=64)
+            for g in range(2):
+                wide[f, g] = keep.tile([P, PACK, w], BF16, name="wide%d_%d" % (f, g), align_bytes=64)
+                mixed[f, g] = keep.tile([P, w, PACK], BF16, name="mixed%d_%d" % (f, g), align_bytes=64)
 
-        def widen(c, g, on_vector):
-            for t in range(PACK):
-                for b in range(WIDTHS[c] // BLOCK):
-                    lo = starts[c] + b * BLOCK
-                    src = r_raw[:, g, t, lo : lo + BLOCK].bitcast(FP8)
-                    dst = wide[c][:, g, t, b * BLOCK : (b + 1) * BLOCK]
-                    sc = r_sc[:, g, t, lo // BLOCK : lo // BLOCK + 1]
-                    if on_vector:
+        def W(f, g, engine="s", ts=(0, 1, 2, 3)):
+            gi, off, w, lo = chunks[f]
+            for t in ts:
+                for b in range(w // BLOCK):
+                    col = lo + b * BLOCK
+                    src = r_raw[:, g, t, col : col + BLOCK].bitcast(FP8)
+                    dst = wide[f, g][:, t, b * BLOCK : (b + 1) * BLOCK]
+                    sc = r_sc[:, g, t, col // BLOCK : col // BLOCK + 1]
+                    if engine == "v":
                         nc.vector.tensor_scalar(out=dst, in0=src, scalar1=sc, scalar2=None, op0=MULT)
                     else:
                         nc.scalar.activation(out=dst, in_=src, func=COPY, scale=sc)
 
-        def mix_r(c, g):
-            nc.vector.tensor_copy(out=mixed[c][:, g], in_=wide[c][:, g].rearrange("p t n -> p n t"))
+        def Mx(f, g):
+            nc.vector.tensor_copy(out=mixed[f, g][:], in_=wide[f, g][:].rearrange("p t n -> p n t"))
 
-        def quant_r(c):
+        def Q(f, g):
+            gi, off, w, lo = chunks[f]
             nc.vector.quantize_mx(
-                out=r_codes[c][:].bitcast(FP8X4),
-                scales=r_planes[c][:],
-                in_=mixed[c][:].rearrange("p g n t -> p (g n t)"),
+                out=r_codes[gi][:, g, off : off + w].bitcast(FP8X4),
+                scales=r_planes[gi][:, g, off : off + w],
+                in_=mixed[f, g][:].rearrange("p n t -> p (n t)"),
             )
+
+        def KS():
+            nc.vector.tensor_copy(
+                out=k_sc[:].rearrange("p (t m) -> p t m", t=PACK), in_=ks_raw[:].rearrange("p (m t) -> p t m", t=PACK)
+            )
+
+        def KW(g):
+            nc.vector.tensor_copy(
+                out=k_codes[:, g, :].rearrange("p (t m) -> p t m", t=PACK).bitcast(I32),
+                in_=k_raw[:, g, :].bitcast(I32).rearrange("p (m t) -> p t m", t=PACK),
+            )
+
+        def VEC():
+            nc.vector.tensor_copy(out=vec[:], in_=vec_bf[:, :, 0:PACK])
 
         kr = {}
 
-        def gain(c):
-            w = WIDTHS[c]
+        def K(f):
+            gi, off, w, lo = chunks[f]
             per = BANK // w
             for b in range(PACK // per):
                 bank = psum.tile([P, per, w], F32, name="bank")
-                kr[c, b] = bank
+                kr[f, b] = bank
                 for i in range(per):
-                    t = b * per + i
+                    cols = slice((b * per + i) * P, (b * per + i + 1) * P)
                     for g in range(2):
-                        cols = slice(t * P, (t + 1) * P)
                         nc.tensor.matmul_mx(
                             out=bank[:, i, :],
                             lhsT=k_codes[:, g, cols].bitcast(FP8X4),
                             lhsT_scale=k_sc[4 * g : P, cols],
-                            rhs=r_codes[c][:, g * w : (g + 1) * w].bitcast(FP8X4),
-                            rhs_scale=r_planes[c][:, g * w : (g + 1) * w],
+                            rhs=r_codes[gi][:, g, off : off + w].bitcast(FP8X4),
+                            rhs_scale=r_planes[gi][:, g, off : off + w],
                             start=(g == 0),
                             stop=(g == 1),
                         )
 
-        def error(c):
-            w = WIDTHS[c]
+        def U(f):
+            gi, off, w, lo = chunks[f]
             per = BANK // w
             for t in range(PACK):
                 nc.vector.scalar_tensor_tensor(
-                    out=u32[c][:, t, :],
-                    in0=v_sb[:, t, starts[c] : starts[c] + w],
+                    out=u32[gi][:, t, off : off + w],
+                    in0=v_sb[:, t, lo : lo + w],
                     scalar=vec[:, 0, t : t + 1],
-                    in1=kr[c, t // per][:, t % per, :],
+                    in1=kr[f, t // per][:, t % per, :],
                     op0=MULT,
                     op1=SUB,
                 )
 
-        def mix_u(c):
-            nc.vector.tensor_copy(out=u_mixed[c][:], in_=u32[c][:].rearrange("p t n -> p n t"))
+        def J(f):
+            gi, off, w, lo = chunks[f]
+            nc.vector.tensor_copy(out=u_mixed[f][:], in_=u32[gi][:, :, off : off + w].rearrange("p t n -> p n t"))
 
-        def quant_u(c):
+        def Pq(f):
+            gi, off, w, lo = chunks[f]
             nc.vector.quantize_mx(
-                out=u_codes[c][:].bitcast(FP8X4),
-                scales=u_planes[c][:],
-                in_=u_mixed[c][:].rearrange("p n t -> p (n t)"),
+                out=u_codes[gi][:, off : off + w].bitcast(FP8X4),
+                scales=u_planes[gi][:, off : off + w],
+                in_=u_mixed[f][:].rearrange("p n t -> p (n t)"),
             )
 
-        def disturbance(c, ts, on_vector):
+        def E(f, ts, engine):
+            gi, off, w, lo = chunks[f]
             for t in ts:
-                if on_vector:
-                    nc.vector.tensor_scalar(
-                        out=eps[c][:, t, :], in0=u32[c][:, t, :], scalar1=vec[:, 1, t : t + 1], scalar2=None, op0=MULT
-                    )
+                src, dst = u32[gi][:, t, off : off + w], eps[gi][:, t, off : off + w]
+                if engine == "v":
+                    nc.vector.tensor_scalar(out=dst, in0=src, scalar1=vec[:, 1, t : t + 1], scalar2=None, op0=MULT)
                 else:
-                    nc.scalar.activation(out=eps[c][:, t, :], in_=u32[c][:, t, :], func=COPY, scale=vec[:, 1, t : t + 1])
+                    nc.scalar.activation(out=dst, in_=src, func=COPY, scale=vec[:, 1, t : t + 1])
 
-        def store_eps(c):
-            nc.sync.dma_start(out=eps_view[:, :, starts[c] : starts[c] + WIDTHS[c]], in_=eps[c][:])
+        def store_eps(gi):
+            nc.sync.dma_start(
+                out=eps_view[:, :, group_start[gi] : group_start[gi] + group_width[gi]], in_=eps[gi][:]
+            )
 
         acc = {}
 
-        def transition(c, b, i):
-            w = WIDTHS[c]
-            s = b * SLICES[c] + i
+        def open_bank(gi, b):
+            acc[gi, b] = psum.tile([P, SLICES[gi], group_width[gi]], F32, name="bank")
+
+        def transition(gi, b, i):
+            s = b * SLICES[gi] + i
             cols = slice(s * P, (s + 1) * P)
             for g in range(2):
                 nc.tensor.matmul_mx(
-                    out=acc[c, b][:, i, :],
+                    out=acc[gi, b][:, i, :],
                     lhsT=t_codes[:, g, cols].bitcast(FP8X4),
                     lhsT_scale=t_sc[4 * g : P, cols],
-                    rhs=r_codes[c][:, g * w : (g + 1) * w].bitcast(FP8X4),
-                    rhs_scale=r_planes[c][:, g * w : (g + 1) * w],
+                    rhs=r_codes[gi][:, g, :].bitcast(FP8X4),
+                    rhs_scale=r_planes[gi][:, g, :],
                     start=(g == 0),
                     stop=False,
                 )
 
-        def observe(c, b, i):
-            w = WIDTHS[c]
-            s = b * SLICES[c] + i
+        def observe(gi, b, i):
+            s = b * SLICES[gi] + i
             cols = slice(s * P, (s + 1) * P)
             nc.tensor.matmul_mx(
-                out=acc[c, b][:, i, :],
+                out=acc[gi, b][:, i, :],
                 lhsT=z_codes[:, cols].bitcast(FP8X4),
                 lhsT_scale=z_sc[:, cols],
-                rhs=u_codes[c][:].bitcast(FP8X4),
-                rhs_scale=u_planes[c][:],
+                rhs=u_codes[gi][:].bitcast(FP8X4),
+                rhs_scale=u_planes[gi][:],
                 start=False,
                 stop=True,
             )
 
-        def early(c):
-            w = WIDTHS[c]
-            per = SLICES[c]
-            for b in range(8 // per):
-                acc[c, b] = psum.tile([P, per, w], F32, name="bank")
-                transition(c, b, 0)
+        def T(gi, banks):
+            for b in banks:
+                open_bank(gi, b)
+                transition(gi, b, 0)
 
-        def late(c, vector_banks):
-            w = WIDTHS[c]
-            per = SLICES[c]
-            for b in range(8 // per):
-                observe(c, b, 0)
-                for i in range(1, per):
-                    transition(c, b, i)
-                    observe(c, b, i)
-                res = keep.tile([P, per, w], F32, name="res%d_%d" % (c, b), align_bytes=64)
-                if b in vector_banks:
-                    nc.vector.tensor_copy(out=res[:], in_=acc[c, b][:])
+        def O(gi, banks, engines):
+            for b, engine in zip(banks, engines):
+                if (gi, b) not in acc:
+                    open_bank(gi, b)
+                    transition(gi, b, 0)
+                observe(gi, b, 0)
+                for i in range(1, SLICES[gi]):
+                    transition(gi, b, i)
+                    observe(gi, b, i)
+                per, w, lo = SLICES[gi], group_width[gi], group_start[gi]
+                res = keep.tile([P, per, w], F32, name="res%d_%d" % (gi, b), align_bytes=64)
+                if engine == "v":
+                    nc.vector.tensor_copy(out=res[:], in_=acc[gi, b][:])
                 else:
-                    nc.scalar.copy(out=res[:], in_=acc[c, b][:])
-                nc.sync.dma_start(
-                    out=prev_view[:, b * per : (b + 1) * per, starts[c] : starts[c] + w], in_=res[:]
-                )
+                    nc.scalar.copy(out=res[:], in_=acc[gi, b][:])
+                nc.sync.dma_start(out=prev_view[:, b * per : (b + 1) * per, lo : lo + w], in_=res[:])
 
-        widen(0, 0, True)
-        widen(0, 1, False)
-        mix_r(0, 0)
-        mix_r(0, 1)
-        widen(1, 0, False)
-        widen(1, 1, False)
-        nc.vector.tensor_copy(
-            out=k_sc[:].rearrange("p (t m) -> p t m", t=PACK), in_=ks_raw[:].rearrange("p (m t) -> p t m", t=PACK)
-        )
-        nc.vector.tensor_copy(
-            out=k_codes[:].rearrange("p g (t m) -> p g t m", t=PACK).bitcast(I32),
-            in_=k_raw[:].bitcast(I32).rearrange("p g (m t) -> p g t m", t=PACK),
-        )
-        quant_r(0)
-        gain(0)
-        mix_r(1, 0)
-        mix_r(1, 1)
-        nc.vector.tensor_copy(out=vec[:], in_=vec_bf[:, :, 0:PACK])
-        widen(2, 0, False)
-        widen(2, 1, False)
-        early(0)
-        for c in range(n_chunks):
-            nxt = c + 1
-            error(c)
-            if nxt < n_chunks:
-                quant_r(nxt)
-                gain(nxt)
-            mix_u(c)
-            disturbance(c, (0, 1), True)
-            quant_u(c)
-            disturbance(c, (2, 3), False)
-            store_eps(c)
-            if c + 3 < n_chunks:
-                widen(c + 3, 0, False)
-            late(c, (0, 2) if c == n_chunks - 1 else ())
-            if nxt < n_chunks:
-                early(nxt)
-            if c + 2 < n_chunks:
-                mix_r(c + 2, 0)
-                mix_r(c + 2, 1)
-            if c + 3 < n_chunks:
-                widen(c + 3, 1, False)
+        W(0, 0, "v", (0, 1))
+        W(0, 0, "s", (2, 3))
+        VEC()
+        Mx(0, 0)
+        W(1, 0, "s", (0, 1))
+        W(0, 1, "s", (0, 1))
+        W(0, 1, "v", (2, 3))
+        Q(0, 0)
+        Mx(0, 1)
+        W(1, 0, "s", (2, 3))
+        W(1, 1)
+        W(2, 0)
+        W(2, 1)
+        KW(0)
+        Q(0, 1)
+        KW(1)
+        KS()
+        K(0)
+        T(0, range(4))
+        Mx(1, 0)
+        Mx(1, 1)
+        U(0)
+        W(3, 0, "s", (0, 1))
+        E(0, (0, 1, 2, 3), "s")
+        store_eps(0)
+        W(3, 0, "s", (2, 3))
+        W(3, 1)
+        Q(1, 0)
+        Q(1, 1)
+        K(1)
+        J(0)
+        Mx(2, 0)
+        Pq(0)
+        O(0, range(4), "ssss")
+        T(1, range(4))
+        U(1)
+        E(1, (0, 1), "s")
+        Q(2, 0)
+        J(1)
+        Mx(2, 1)
+        Pq(1)
+        Q(2, 1)
+        O(1, range(1), "s")
+        K(2)
+        E(1, (2, 3), "v")
+        store_eps(1)
+        Mx(3, 0)
+        Mx(3, 1)
+        Q(3, 0)
+        U(2)
+        O(1, range(1, 3), "ss")
+        E(2, (0, 1, 2, 3), "s")
+        store_eps(2)
+        O(1, range(3, 4), "v")
+        Q(3, 1)
+        J(2)
+        T(2, range(2))
+        K(3)
+        T(2, range(2, 4))
+        Pq(2)
+        U(3)
+        J(3)
+        E(3, (0, 1), "v")
+        O(2, range(3), "sss")
+        Pq(3)
+        E(3, (2, 3), "v")
+        store_eps(3)
+        O(2, range(3, 4), "v")
+        T(3, range(4))
+        O(3, range(4), "vsvs")

@@ -90,16 +90,16 @@ def tile_durbinkoopmandisturbancesmootherstep_d1p_kernel(
         def load_vec(queue, i, src):
             queue.dma_start(out=vec_bf[:, i, 0:PACK], in_=src.rearrange("(p t) -> p t", t=PACK))
 
-        for q in range(4):
-            load_ks(nc.gpsimd, q)
         nc.sync.dma_start(out=r_sc[:], in_=r_scale.rearrange("(g p t) j -> p g t j", p=P, t=PACK))
         nc.sync.dma_start(out=r_raw[:, 0], in_=r_view[:, 0])
         nc.sync.dma_start(out=r_raw[:, 1], in_=r_view[:, 1])
         nc.sync.dma_start(out=k_raw[:].bitcast(I32), in_=k_dram)
+        for q in range(4):
+            load_ks(nc.scalar, q)
         nc.sync.dma_start(out=v_sb[:, :, 0:512], in_=v_view[:, :, 0:512])
-        load_vec(nc.scalar, 0, finv)
-        load_vec(nc.scalar, 1, h)
         nc.sync.dma_start(out=t_codes[:].bitcast(I32), in_=t_dram)
+        load_vec(nc.sync, 0, finv)
+        load_vec(nc.sync, 1, h)
         for q in range(4):
             load_ts(nc.sync, q)
         nc.sync.dma_start(out=z_codes[:].bitcast(I32), in_=z_dram)
@@ -136,7 +136,10 @@ def tile_durbinkoopmandisturbancesmootherstep_d1p_kernel(
                         nc.scalar.activation(out=dst, in_=src, func=COPY, scale=sc)
 
         def Mx(f, g):
-            nc.vector.tensor_copy(out=mixed[f, g][:], in_=wide[f, g][:].rearrange("p t n -> p n t"))
+            nc.vector.tensor_copy(
+                out=mixed[f, g][:].rearrange("p (c i) t -> p c t i", i=4),
+                in_=wide[f, g][:].rearrange("p t (c i) -> p c t i", i=4),
+            )
 
         def Q(f, g):
             gi, off, w, lo = chunks[f]
@@ -157,8 +160,8 @@ def tile_durbinkoopmandisturbancesmootherstep_d1p_kernel(
                 in_=k_raw[:, g, :].bitcast(I32).rearrange("p (m t) -> p t m", t=PACK),
             )
 
-        def VEC():
-            nc.vector.tensor_copy(out=vec[:], in_=vec_bf[:, :, 0:PACK])
+        def VEC(i):
+            nc.vector.tensor_copy(out=vec[:, i, :], in_=vec_bf[:, i, 0:PACK])
 
         kr = {}
 
@@ -274,11 +277,24 @@ def tile_durbinkoopmandisturbancesmootherstep_d1p_kernel(
                     nc.scalar.copy(out=res[:], in_=acc[gi, b][:])
                 nc.sync.dma_start(out=prev_view[:, b * per : (b + 1) * per, lo : lo + w], in_=res[:])
 
+        def WARM(n):
+            bank = psum.tile([P, BANK], F32, name="bank")
+            src = wide[0, 0]
+            for i in range(n):
+                nc.tensor.matmul(
+                    bank[:],
+                    lhsT=src[:, 0, 0:P],
+                    rhs=src[:, 0:2, :].rearrange("p t n -> p (t n)"),
+                    start=True,
+                    stop=True,
+                )
+
         W(0, 0, "v", (0, 1))
         W(0, 0, "s", (2, 3))
-        VEC()
-        Mx(0, 0)
+        WARM(10)
         W(1, 0, "s", (0, 1))
+        Mx(0, 0)
+        KS()
         W(0, 1, "s", (0, 1))
         W(0, 1, "v", (2, 3))
         Q(0, 0)
@@ -290,57 +306,54 @@ def tile_durbinkoopmandisturbancesmootherstep_d1p_kernel(
         KW(0)
         Q(0, 1)
         KW(1)
-        KS()
         K(0)
         T(0, range(4))
         Mx(1, 0)
+        VEC(0)
         Mx(1, 1)
         U(0)
+        VEC(1)
         W(3, 0, "s", (0, 1))
         E(0, (0, 1, 2, 3), "s")
         store_eps(0)
         W(3, 0, "s", (2, 3))
         W(3, 1)
         Q(1, 0)
+        J(0)
         Q(1, 1)
         K(1)
-        J(0)
-        Mx(2, 0)
         Pq(0)
         O(0, range(4), "ssss")
-        T(1, range(4))
-        U(1)
-        E(1, (0, 1), "s")
-        Q(2, 0)
-        J(1)
+        Mx(2, 0)
         Mx(2, 1)
-        Pq(1)
+        U(1)
+        T(1, range(2))
+        Q(2, 0)
         Q(2, 1)
-        O(1, range(1), "s")
         K(2)
-        E(1, (2, 3), "v")
+        J(1)
+        E(1, (0, 1), "v")
+        E(1, (2, 3), "s")
         store_eps(1)
+        Pq(1)
+        T(1, range(2, 3))
+        O(1, range(4), "ssss")
         Mx(3, 0)
+        U(2)
         Mx(3, 1)
         Q(3, 0)
-        U(2)
-        O(1, range(1, 3), "ss")
-        E(2, (0, 1, 2, 3), "s")
-        store_eps(2)
-        O(1, range(3, 4), "v")
-        Q(3, 1)
         J(2)
-        T(2, range(2))
+        Q(3, 1)
         K(3)
-        T(2, range(2, 4))
+        E(2, (0, 1), "v")
         Pq(2)
+        E(2, (2, 3), "s")
+        store_eps(2)
+        O(2, range(4), "ssss")
         U(3)
         J(3)
         E(3, (0, 1), "v")
-        O(2, range(3), "sss")
         Pq(3)
         E(3, (2, 3), "v")
         store_eps(3)
-        O(2, range(3, 4), "v")
-        T(3, range(4))
         O(3, range(4), "vsvs")

@@ -22,7 +22,7 @@ BLOCK = 128
 BANK = 512
 
 GROUPS = ((256,), (256,), (256,), (256,))
-SLICES = (2, 2, 2, 2)
+SLICES = (2, 2, 2, 1)
 
 
 def tile_durbinkoopmandisturbancesmootherstep_d1p_kernel(
@@ -52,19 +52,19 @@ def tile_durbinkoopmandisturbancesmootherstep_d1p_kernel(
         psum = ctx.enter_context(tc.psum_pool(name="psum", bufs=8))
         ctx.enter_context(tc.manual_schedule())
 
-        r_raw = keep.tile([P, 2, PACK, M], U8, name="r_raw", align_bytes=64)
-        r_sc = keep.tile([P, 2, PACK, M // BLOCK], F32, name="r_sc", align_bytes=64)
-        v_sb = keep.tile([P, PACK, M], BF16, name="v_sb", align_bytes=64)
-        vec_bf = keep.tile([P, 2, 16], BF16, name="vec_bf", align_bytes=64)
-        vec = keep.tile([P, 2, PACK], F32, name="vec", align_bytes=64)
-        k_raw = keep.tile([P, 2, P_OBS], U32, name="k_raw", align_bytes=64)
-        k_codes = keep.tile([P, 2, P_OBS], U32, name="k_codes", align_bytes=64)
-        ks_raw = keep.tile([P, P_OBS], U8, name="ks_raw", align_bytes=64)
-        k_sc = keep.tile([P, P_OBS], U8, name="k_sc", align_bytes=64)
-        t_codes = keep.tile([P, 2, S], U32, name="t_codes", align_bytes=64)
-        z_codes = keep.tile([P, S], U32, name="z_codes", align_bytes=64)
-        t_sc = keep.tile([P, S], U8, name="t_sc", align_bytes=64)
-        z_sc = keep.tile([P, S], U8, name="z_sc", align_bytes=64)
+        r_raw = keep.tile([P, 2, PACK, M], U8, name="r_raw", align_bytes=256)
+        r_sc = keep.tile([P, 2, PACK, M // BLOCK], F32, name="r_sc", align_bytes=256)
+        v_sb = keep.tile([P, PACK, M], BF16, name="v_sb", align_bytes=256)
+        vec_bf = keep.tile([P, 2, 16], BF16, name="vec_bf", align_bytes=256)
+        vec = keep.tile([P, 2, PACK], F32, name="vec", align_bytes=256)
+        k_raw = keep.tile([P, 2, P_OBS], U32, name="k_raw", align_bytes=256)
+        k_codes = keep.tile([P, 2, P_OBS], U32, name="k_codes", align_bytes=256)
+        ks_raw = keep.tile([P, P_OBS], U8, name="ks_raw", align_bytes=256)
+        k_sc = keep.tile([P, P_OBS], U8, name="k_sc", align_bytes=256)
+        t_codes = keep.tile([P, 2, S], U32, name="t_codes", align_bytes=256)
+        z_codes = keep.tile([P, S], U32, name="z_codes", align_bytes=256)
+        t_sc = keep.tile([P, S], U8, name="t_sc", align_bytes=256)
+        z_sc = keep.tile([P, S], U8, name="z_sc", align_bytes=256)
 
         for plane in (ks_raw, t_sc, z_sc):
             nc.vector.memset(plane[:].bitcast(U32), 0)
@@ -92,17 +92,17 @@ def tile_durbinkoopmandisturbancesmootherstep_d1p_kernel(
 
         nc.sync.dma_start(out=r_sc[:], in_=r_scale.rearrange("(g p t) j -> p g t j", p=P, t=PACK))
         nc.sync.dma_start(out=r_raw[:, 0], in_=r_view[:, 0])
+        for q in range(4):
+            load_ks(nc.sync, q)
         nc.sync.dma_start(out=r_raw[:, 1], in_=r_view[:, 1])
         nc.sync.dma_start(out=k_raw[:].bitcast(I32), in_=k_dram)
-        for q in range(4):
-            load_ks(nc.scalar, q)
-        nc.sync.dma_start(out=v_sb[:, :, 0:512], in_=v_view[:, :, 0:512])
         nc.sync.dma_start(out=t_codes[:].bitcast(I32), in_=t_dram)
-        load_vec(nc.sync, 0, finv)
-        load_vec(nc.sync, 1, h)
+        load_vec(nc.scalar, 0, finv)
         for q in range(4):
             load_ts(nc.sync, q)
+        nc.sync.dma_start(out=v_sb[:, :, 0:512], in_=v_view[:, :, 0:512])
         nc.sync.dma_start(out=z_codes[:].bitcast(I32), in_=z_dram)
+        load_vec(nc.sync, 1, h)
         for q in range(4):
             load_zs(nc.sync, q)
         nc.sync.dma_start(out=v_sb[:, :, 512:1024], in_=v_view[:, :, 512:1024])
@@ -110,17 +110,17 @@ def tile_durbinkoopmandisturbancesmootherstep_d1p_kernel(
         wide, mixed, r_codes, r_planes = {}, {}, [], []
         u32, u_mixed, u_codes, u_planes, eps = [], {}, [], [], []
         for gi, w in enumerate(group_width):
-            r_codes.append(keep.tile([P, 2, w], U32, name="r_codes%d" % gi, align_bytes=64))
-            r_planes.append(keep.tile([P, 2, w], U8, name="r_planes%d" % gi, align_bytes=64))
-            u32.append(keep.tile([P, PACK, w], F32, name="u32_%d" % gi, align_bytes=64))
-            u_codes.append(keep.tile([P, w], U32, name="u_codes%d" % gi, align_bytes=64))
-            u_planes.append(keep.tile([P, w], U8, name="u_planes%d" % gi, align_bytes=64))
-            eps.append(keep.tile([P, PACK, w], F32, name="eps%d" % gi, align_bytes=64))
+            r_codes.append(keep.tile([P, 2, w], U32, name="r_codes%d" % gi, align_bytes=256))
+            r_planes.append(keep.tile([P, 2, w], U8, name="r_planes%d" % gi, align_bytes=256))
+            u32.append(keep.tile([P, PACK, w], F32, name="u32_%d" % gi, align_bytes=256))
+            u_codes.append(keep.tile([P, w], U32, name="u_codes%d" % gi, align_bytes=256))
+            u_planes.append(keep.tile([P, w], U8, name="u_planes%d" % gi, align_bytes=256))
+            eps.append(keep.tile([P, PACK, w], F32, name="eps%d" % gi, align_bytes=256))
         for f, (gi, off, w, lo) in enumerate(chunks):
-            u_mixed[f] = keep.tile([P, w, PACK], BF16, name="u_mixed%d" % f, align_bytes=64)
+            u_mixed[f] = keep.tile([P, w, PACK], BF16, name="u_mixed%d" % f, align_bytes=256)
             for g in range(2):
-                wide[f, g] = keep.tile([P, PACK, w], BF16, name="wide%d_%d" % (f, g), align_bytes=64)
-                mixed[f, g] = keep.tile([P, w, PACK], BF16, name="mixed%d_%d" % (f, g), align_bytes=64)
+                wide[f, g] = keep.tile([P, PACK, w], BF16, name="wide%d_%d" % (f, g), align_bytes=256)
+                mixed[f, g] = keep.tile([P, w, PACK], BF16, name="mixed%d_%d" % (f, g), align_bytes=256)
 
         def W(f, g, engine="s", ts=(0, 1, 2, 3)):
             gi, off, w, lo = chunks[f]
@@ -135,11 +135,13 @@ def tile_durbinkoopmandisturbancesmootherstep_d1p_kernel(
                     else:
                         nc.scalar.activation(out=dst, in_=src, func=COPY, scale=sc)
 
-        def Mx(f, g):
-            nc.vector.tensor_copy(
-                out=mixed[f, g][:].rearrange("p (c i) t -> p c t i", i=4),
-                in_=wide[f, g][:].rearrange("p t (c i) -> p c t i", i=4),
-            )
+        def Mx(f, g, engine="v"):
+            dst = mixed[f, g][:].rearrange("p (c i) t -> p c t i", i=4)
+            src = wide[f, g][:].rearrange("p t (c i) -> p c t i", i=4)
+            if engine == "v":
+                nc.vector.tensor_copy(out=dst, in_=src)
+            else:
+                nc.scalar.copy(out=dst, in_=src)
 
         def Q(f, g):
             gi, off, w, lo = chunks[f]
@@ -154,10 +156,10 @@ def tile_durbinkoopmandisturbancesmootherstep_d1p_kernel(
                 out=k_sc[:].rearrange("p (t m) -> p t m", t=PACK), in_=ks_raw[:].rearrange("p (m t) -> p t m", t=PACK)
             )
 
-        def KW(g):
+        def KW(half):
             nc.vector.tensor_copy(
-                out=k_codes[:, g, :].rearrange("p (t m) -> p t m", t=PACK).bitcast(I32),
-                in_=k_raw[:, g, :].bitcast(I32).rearrange("p (m t) -> p t m", t=PACK),
+                out=k_codes[:].bitcast(I32).rearrange("p g (t m) -> p g t m", t=PACK)[:, :, 2 * half : 2 * half + 2, :],
+                in_=k_raw[:].bitcast(I32).rearrange("p g (m t) -> p g t m", t=PACK)[:, :, 2 * half : 2 * half + 2, :],
             )
 
         def VEC(i):
@@ -270,7 +272,7 @@ def tile_durbinkoopmandisturbancesmootherstep_d1p_kernel(
                     transition(gi, b, i)
                     observe(gi, b, i)
                 per, w, lo = SLICES[gi], group_width[gi], group_start[gi]
-                res = keep.tile([P, per, w], F32, name="res%d_%d" % (gi, b), align_bytes=64)
+                res = keep.tile([P, per, w], F32, name="res%d_%d" % (gi, b), align_bytes=256)
                 if engine == "v":
                     nc.vector.tensor_copy(out=res[:], in_=acc[gi, b][:])
                 else:
@@ -291,7 +293,7 @@ def tile_durbinkoopmandisturbancesmootherstep_d1p_kernel(
 
         W(0, 0, "v", (0, 1))
         W(0, 0, "s", (2, 3))
-        WARM(10)
+        WARM(8)
         W(1, 0, "s", (0, 1))
         Mx(0, 0)
         KS()
@@ -308,52 +310,50 @@ def tile_durbinkoopmandisturbancesmootherstep_d1p_kernel(
         KW(1)
         K(0)
         T(0, range(4))
-        Mx(1, 0)
         VEC(0)
+        Mx(1, 0)
         Mx(1, 1)
-        U(0)
-        VEC(1)
-        W(3, 0, "s", (0, 1))
-        E(0, (0, 1, 2, 3), "s")
-        store_eps(0)
-        W(3, 0, "s", (2, 3))
-        W(3, 1)
         Q(1, 0)
-        J(0)
         Q(1, 1)
         K(1)
+        U(0)
+        VEC(1)
+        W(3, 0)
+        J(0)
+        E(0, (0, 1, 2, 3), "s")
+        store_eps(0)
+        W(3, 1)
+        T(1, range(2))
         Pq(0)
         O(0, range(4), "ssss")
         Mx(2, 0)
         Mx(2, 1)
         U(1)
-        T(1, range(2))
         Q(2, 0)
         Q(2, 1)
         K(2)
         J(1)
-        E(1, (0, 1), "v")
-        E(1, (2, 3), "s")
+        E(1, (0, 1, 2, 3), "s")
         store_eps(1)
         Pq(1)
         T(1, range(2, 3))
         O(1, range(4), "ssss")
         Mx(3, 0)
-        U(2)
         Mx(3, 1)
+        U(2)
         Q(3, 0)
-        J(2)
         Q(3, 1)
+        T(2, range(2))
         K(3)
-        E(2, (0, 1), "v")
-        Pq(2)
-        E(2, (2, 3), "s")
+        J(2)
+        E(2, (0, 1, 2, 3), "s")
         store_eps(2)
+        Pq(2)
         O(2, range(4), "ssss")
         U(3)
         J(3)
-        E(3, (0, 1), "v")
         Pq(3)
+        E(3, (0, 1), "s")
         E(3, (2, 3), "v")
         store_eps(3)
-        O(3, range(4), "vsvs")
+        O(3, range(8), "vsvsvsvs")

from contextlib import ExitStack

import concourse.mybir as mybir

S, P_OBS, M = 1024, 512, 1024
FLOPS = 2 * M * (2 * S * P_OBS + S * S)

F32 = mybir.dt.float32
BF16 = mybir.dt.bfloat16
I32 = mybir.dt.int32
U32 = mybir.dt.uint32
U8 = mybir.dt.uint8
FP8 = mybir.dt.float8_e4m3fn
FP8X4 = mybir.dt.float8_e4m3fn_x4
COPY = mybir.ActivationFunctionType.Copy
MULT = mybir.AluOpType.mult
SUB = mybir.AluOpType.subtract

P = 128
PACK = 4
BLOCK = 128
BANK = 512

GROUPS = ((256,), (256,), (256,), (256,))
SLICES = (2, 2, 2, 1)


def tile_durbinkoopmandisturbancesmootherstep_d1p_kernel(
    tc, r_bytes, r_scale, v, finv, k_words, k_scales, z_words, z_scales, t_words, t_scales, h, out_0, out_1
):
    nc = tc.nc
    chunks = []
    group_start, group_width = [], []
    at = 0
    for gi, parts in enumerate(GROUPS):
        group_start.append(at)
        group_width.append(sum(parts))
        off = 0
        for w in parts:
            chunks.append((gi, off, w, at))
            off += w
            at += w
    n_chunks = len(chunks)

    r_view = r_bytes.rearrange("(g p t) m -> p g t m", p=P, t=PACK)
    v_view = v.rearrange("(p t) m -> p t m", t=PACK)
    eps_view = out_1.rearrange("(p t) m -> p t m", t=PACK)
    prev_view = out_0.rearrange("(s p) m -> p s m", p=P)

    with ExitStack() as ctx:
        keep = ctx.enter_context(tc.tile_pool(name="keep", bufs=1))
        psum = ctx.enter_context(tc.psum_pool(name="psum", bufs=8))
        ctx.enter_context(tc.manual_schedule())

        r_raw = keep.tile([P, 2, PACK, M], U8, name="r_raw", align_bytes=256)
        r_sc = keep.tile([P, 2, PACK, M // BLOCK], F32, name="r_sc", align_bytes=256)
        v_sb = keep.tile([P, PACK, M], BF16, name="v_sb", align_bytes=256)
        vec_bf = keep.tile([P, 2, 16], BF16, name="vec_bf", align_bytes=256)
        vec = keep.tile([P, 2, PACK], F32, name="vec", align_bytes=256)
        k_raw = keep.tile([P, 2, P_OBS], U32, name="k_raw", align_bytes=256)
        k_codes = keep.tile([P, 2, P_OBS], U32, name="k_codes", align_bytes=256)
        ks_raw = keep.tile([P, P_OBS], U8, name="ks_raw", align_bytes=256)
        k_sc = keep.tile([P, P_OBS], U8, name="k_sc", align_bytes=256)
        t_codes = keep.tile([P, 2, S], U32, name="t_codes", align_bytes=256)
        z_codes = keep.tile([P, S], U32, name="z_codes", align_bytes=256)
        t_sc = keep.tile([P, S], U8, name="t_sc", align_bytes=256)
        z_sc = keep.tile([P, S], U8, name="z_sc", align_bytes=256)

        for plane in (ks_raw, t_sc, z_sc):
            nc.vector.memset(plane[:].bitcast(U32), 0)
        k_dram = k_words.rearrange("g p n t -> p g (n t)").bitcast(I32)
        t_dram = t_words.rearrange("g p n t -> p g (n t)").bitcast(I32)
        z_dram = z_words[0].rearrange("p n t -> p (n t)").bitcast(I32)

        def load_ks(queue, q):
            queue.dma_start(
                out=ks_raw[32 * q : 32 * q + 8, :].bitcast(I32), in_=k_scales[:, 4 * q : 4 * q + 4, :].bitcast(I32)
            )

        def load_ts(queue, q):
            queue.dma_start(
                out=t_sc[32 * q : 32 * q + 8, :].bitcast(I32), in_=t_scales[:, 4 * q : 4 * q + 4, :].bitcast(I32)
            )

        def load_zs(queue, q):
            queue.dma_start(
                out=z_sc[32 * q : 32 * q + 4, :].bitcast(I32), in_=z_scales[0, 4 * q : 4 * q + 4, :].bitcast(I32)
            )

        def load_vec(queue, i, src):
            queue.dma_start(out=vec_bf[:, i, 0:PACK], in_=src.rearrange("(p t) -> p t", t=PACK))

        nc.sync.dma_start(out=r_sc[:], in_=r_scale.rearrange("(g p t) j -> p g t j", p=P, t=PACK))
        nc.sync.dma_start(out=r_raw[:, 0], in_=r_view[:, 0])
        for q in range(4):
            load_ks(nc.sync, q)
        nc.sync.dma_start(out=r_raw[:, 1], in_=r_view[:, 1])
        nc.sync.dma_start(out=k_raw[:].bitcast(I32), in_=k_dram)
        nc.sync.dma_start(out=t_codes[:].bitcast(I32), in_=t_dram)
        load_vec(nc.scalar, 0, finv)
        for q in range(4):
            load_ts(nc.sync, q)
        nc.sync.dma_start(out=v_sb[:, :, 0:512], in_=v_view[:, :, 0:512])
        nc.sync.dma_start(out=z_codes[:].bitcast(I32), in_=z_dram)
        load_vec(nc.sync, 1, h)
        for q in range(4):
            load_zs(nc.sync, q)
        nc.sync.dma_start(out=v_sb[:, :, 512:1024], in_=v_view[:, :, 512:1024])

        wide, mixed, r_codes, r_planes = {}, {}, [], []
        u32, u_mixed, u_codes, u_planes, eps = [], {}, [], [], []
        for gi, w in enumerate(group_width):
            r_codes.append(keep.tile([P, 2, w], U32, name="r_codes%d" % gi, align_bytes=256))
            r_planes.append(keep.tile([P, 2, w], U8, name="r_planes%d" % gi, align_bytes=256))
            u32.append(keep.tile([P, PACK, w], F32, name="u32_%d" % gi, align_bytes=256))
            u_codes.append(keep.tile([P, w], U32, name="u_codes%d" % gi, align_bytes=256))
            u_planes.append(keep.tile([P, w], U8, name="u_planes%d" % gi, align_bytes=256))
            eps.append(keep.tile([P, PACK, w], F32, name="eps%d" % gi, align_bytes=256))
        for f, (gi, off, w, lo) in enumerate(chunks):
            u_mixed[f] = keep.tile([P, w, PACK], BF16, name="u_mixed%d" % f, align_bytes=256)
            for g in range(2):
                wide[f, g] = keep.tile([P, PACK, w], BF16, name="wide%d_%d" % (f, g), align_bytes=256)
                mixed[f, g] = keep.tile([P, w, PACK], BF16, name="mixed%d_%d" % (f, g), align_bytes=256)

        def W(f, g, engine="s", ts=(0, 1, 2, 3)):
            gi, off, w, lo = chunks[f]
            for t in ts:
                for b in range(w // BLOCK):
                    col = lo + b * BLOCK
                    src = r_raw[:, g, t, col : col + BLOCK].bitcast(FP8)
                    dst = wide[f, g][:, t, b * BLOCK : (b + 1) * BLOCK]
                    sc = r_sc[:, g, t, col // BLOCK : col // BLOCK + 1]
                    if engine == "v":
                        nc.vector.tensor_scalar(out=dst, in0=src, scalar1=sc, scalar2=None, op0=MULT)
                    else:
                        nc.scalar.activation(out=dst, in_=src, func=COPY, scale=sc)

        def Mx(f, g, engine="v"):
            dst = mixed[f, g][:].rearrange("p (c i) t -> p c t i", i=4)
            src = wide[f, g][:].rearrange("p t (c i) -> p c t i", i=4)
            if engine == "v":
                nc.vector.tensor_copy(out=dst, in_=src)
            else:
                nc.scalar.copy(out=dst, in_=src)

        def Q(f, g):
            gi, off, w, lo = chunks[f]
            nc.vector.quantize_mx(
                out=r_codes[gi][:, g, off : off + w].bitcast(FP8X4),
                scales=r_planes[gi][:, g, off : off + w],
                in_=mixed[f, g][:].rearrange("p n t -> p (n t)"),
            )

        def KS():
            nc.vector.tensor_copy(
                out=k_sc[:].rearrange("p (t m) -> p t m", t=PACK), in_=ks_raw[:].rearrange("p (m t) -> p t m", t=PACK)
            )

        def KW(half):
            nc.vector.tensor_copy(
                out=k_codes[:].bitcast(I32).rearrange("p g (t m) -> p g t m", t=PACK)[:, :, 2 * half : 2 * half + 2, :],
                in_=k_raw[:].bitcast(I32).rearrange("p g (m t) -> p g t m", t=PACK)[:, :, 2 * half : 2 * half + 2, :],
            )

        def VEC(i):
            nc.vector.tensor_copy(out=vec[:, i, :], in_=vec_bf[:, i, 0:PACK])

        kr = {}

        def K(f):
            gi, off, w, lo = chunks[f]
            per = BANK // w
            for b in range(PACK // per):
                bank = psum.tile([P, per, w], F32, name="bank")
                kr[f, b] = bank
                for i in range(per):
                    cols = slice((b * per + i) * P, (b * per + i + 1) * P)
                    for g in range(2):
                        nc.tensor.matmul_mx(
                            out=bank[:, i, :],
                            lhsT=k_codes[:, g, cols].bitcast(FP8X4),
                            lhsT_scale=k_sc[4 * g : P, cols],
                            rhs=r_codes[gi][:, g, off : off + w].bitcast(FP8X4),
                            rhs_scale=r_planes[gi][:, g, off : off + w],
                            start=(g == 0),
                            stop=(g == 1),
                        )

        def U(f):
            gi, off, w, lo = chunks[f]
            per = BANK // w
            for t in range(PACK):
                nc.vector.scalar_tensor_tensor(
                    out=u32[gi][:, t, off : off + w],
                    in0=v_sb[:, t, lo : lo + w],
                    scalar=vec[:, 0, t : t + 1],
                    in1=kr[f, t // per][:, t % per, :],
                    op0=MULT,
                    op1=SUB,
                )

        def J(f):
            gi, off, w, lo = chunks[f]
            nc.vector.tensor_copy(out=u_mixed[f][:], in_=u32[gi][:, :, off : off + w].rearrange("p t n -> p n t"))

        def Pq(f):
            gi, off, w, lo = chunks[f]
            nc.vector.quantize_mx(
                out=u_codes[gi][:, off : off + w].bitcast(FP8X4),
                scales=u_planes[gi][:, off : off + w],
                in_=u_mixed[f][:].rearrange("p n t -> p (n t)"),
            )

        def E(f, ts, engine):
            gi, off, w, lo = chunks[f]
            for t in ts:
                src, dst = u32[gi][:, t, off : off + w], eps[gi][:, t, off : off + w]
                if engine == "v":
                    nc.vector.tensor_scalar(out=dst, in0=src, scalar1=vec[:, 1, t : t + 1], scalar2=None, op0=MULT)
                else:
                    nc.scalar.activation(out=dst, in_=src, func=COPY, scale=vec[:, 1, t : t + 1])

        def store_eps(gi):
            nc.sync.dma_start(
                out=eps_view[:, :, group_start[gi] : group_start[gi] + group_width[gi]], in_=eps[gi][:]
            )

        acc = {}

        def open_bank(gi, b):
            acc[gi, b] = psum.tile([P, SLICES[gi], group_width[gi]], F32, name="bank")

        def transition(gi, b, i):
            s = b * SLICES[gi] + i
            cols = slice(s * P, (s + 1) * P)
            for g in range(2):
                nc.tensor.matmul_mx(
                    out=acc[gi, b][:, i, :],
                    lhsT=t_codes[:, g, cols].bitcast(FP8X4),
                    lhsT_scale=t_sc[4 * g : P, cols],
                    rhs=r_codes[gi][:, g, :].bitcast(FP8X4),
                    rhs_scale=r_planes[gi][:, g, :],
                    start=(g == 0),
                    stop=False,
                )

        def observe(gi, b, i):
            s = b * SLICES[gi] + i
            cols = slice(s * P, (s + 1) * P)
            nc.tensor.matmul_mx(
                out=acc[gi, b][:, i, :],
                lhsT=z_codes[:, cols].bitcast(FP8X4),
                lhsT_scale=z_sc[:, cols],
                rhs=u_codes[gi][:].bitcast(FP8X4),
                rhs_scale=u_planes[gi][:],
                start=False,
                stop=True,
            )

        def T(gi, banks):
            for b in banks:
                open_bank(gi, b)
                transition(gi, b, 0)

        def O(gi, banks, engines):
            for b, engine in zip(banks, engines):
                if (gi, b) not in acc:
                    open_bank(gi, b)
                    transition(gi, b, 0)
                observe(gi, b, 0)
                for i in range(1, SLICES[gi]):
                    transition(gi, b, i)
                    observe(gi, b, i)
                per, w, lo = SLICES[gi], group_width[gi], group_start[gi]
                res = keep.tile([P, per, w], F32, name="res%d_%d" % (gi, b), align_bytes=256)
                if engine == "v":
                    nc.vector.tensor_copy(out=res[:], in_=acc[gi, b][:])
                else:
                    nc.scalar.copy(out=res[:], in_=acc[gi, b][:])
                nc.sync.dma_start(out=prev_view[:, b * per : (b + 1) * per, lo : lo + w], in_=res[:])

        def WARM(n):
            bank = psum.tile([P, BANK], F32, name="bank")
            src = wide[0, 0]
            for i in range(n):
                nc.tensor.matmul(
                    bank[:],
                    lhsT=src[:, 0, 0:P],
                    rhs=src[:, 0:2, :].rearrange("p t n -> p (t n)"),
                    start=True,
                    stop=True,
                )

        W(0, 0, "v", (0, 1))
        W(0, 0, "s", (2, 3))
        WARM(8)
        W(1, 0, "s", (0, 1))
        Mx(0, 0)
        KS()
        W(0, 1, "s", (0, 1))
        W(0, 1, "v", (2, 3))
        Q(0, 0)
        Mx(0, 1)
        W(1, 0, "s", (2, 3))
        W(1, 1)
        W(2, 0)
        W(2, 1)
        KW(0)
        Q(0, 1)
        KW(1)
        K(0)
        T(0, range(4))
        VEC(0)
        Mx(1, 0)
        Mx(1, 1)
        Q(1, 0)
        Q(1, 1)
        K(1)
        U(0)
        VEC(1)
        W(3, 0)
        J(0)
        E(0, (0, 1, 2, 3), "s")
        store_eps(0)
        W(3, 1)
        T(1, range(2))
        Pq(0)
        O(0, range(4), "ssss")
        Mx(2, 0)
        Mx(2, 1)
        U(1)
        Q(2, 0)
        Q(2, 1)
        K(2)
        J(1)
        E(1, (0, 1, 2, 3), "s")
        store_eps(1)
        Pq(1)
        T(1, range(2, 3))
        O(1, range(4), "ssss")
        Mx(3, 0)
        Mx(3, 1)
        U(2)
        Q(3, 0)
        Q(3, 1)
        T(2, range(2))
        K(3)
        J(2)
        E(2, (0, 1, 2, 3), "s")
        store_eps(2)
        Pq(2)
        O(2, range(4), "ssss")
        U(3)
        J(3)
        Pq(3)
        E(3, (0, 1), "s")
        E(3, (2, 3), "v")
        store_eps(3)
        O(3, range(8), "vsvsvsvs")
